import numpy as np
import ml_dtypes


def mxq(x, axis, fmt="e4m3"):
    dtype, down = {"e4m3": (ml_dtypes.float8_e4m3fn, 7), "e5m2": (ml_dtypes.float8_e5m2, 14)}[fmt]
    v = np.moveaxis(np.asarray(x, np.float32).astype(ml_dtypes.bfloat16).astype(np.float64), axis, -1)
    blocks = v.reshape(v.shape[:-1] + (-1, 32))
    amax = np.abs(blocks).max(-1, keepdims=True)
    byte = np.maximum(np.where(amax > 0, np.frexp(amax)[1] - 1 + 127, 0) - down, 1)
    scale = np.exp2(byte - 127.0)
    codes = (blocks / scale).astype(np.float32).astype(dtype).astype(np.float64)
    return np.moveaxis((codes * scale).reshape(v.shape), -1, axis)


WIDE = False


def mx_kscale(k):
    if not WIDE:
        return np.ones(k)
    levels = np.array([10, -10, 5, -5, 0])
    if k % 512:
        return np.exp2(np.random.permutation(np.resize(levels, k // 32))).repeat(32)
    a = np.empty((k // 512, 16))
    for p in range(k // 512):
        a[p, :8] = np.random.permutation(np.resize(levels, 8))
        for g in range(8):
            far = levels[np.abs(levels - a[p, g]) >= 10]
            a[p, g + 8] = far[np.random.randint(len(far))]
    return np.exp2(a.ravel()).repeat(32)


def f64(x):
    return np.asarray(x).astype(np.float64)


def striped(idx):
    return np.tile(idx.reshape(-1, 16).T, (8, 1)).astype(np.uint16)


def unstriped(offs):
    return offs[:16].T.reshape(-1).astype(np.int64)


def striped8(idx):
    return np.concatenate([x.reshape(-1, 16).T for x in idx]).astype(np.uint16)


def runs(offs, k):
    lists = np.stack([offs[16 * r : 16 * r + 16].T.reshape(-1) for r in range(8)]).astype(np.int64)
    return lists[np.arange(k) % 512 // 64]


def pack_weight(w):
    k, n = w.shape
    w = f64(np.asarray(w, np.float32).astype(ml_dtypes.bfloat16)).reshape(k // 32, 32, n)
    amax = np.abs(w).max(1)
    byte = np.clip(np.where(amax > 0, np.frexp(amax)[1] - 1 + 127 - 7, 1), 1, 254)
    scaled = (w * np.exp2(127.0 - byte)[:, None, :]).reshape(k, n).astype(np.float32)
    words = np.ascontiguousarray(scaled.reshape(k // 512, 128, 4, n).transpose(0, 1, 3, 2)).astype(ml_dtypes.float8_e4m3fn).view(np.uint8)
    return words, np.ascontiguousarray(byte.astype(np.uint8).reshape(k // 512, 16, n))


def unpack_weight(words, scales):
    g, p, n, _ = words.shape
    vals = np.ascontiguousarray(words).view(ml_dtypes.float8_e4m3fn).astype(np.float64) * np.repeat(np.exp2(scales.astype(np.float64) - 127.0), 8, axis=1)[..., None]
    return vals.transpose(0, 1, 3, 2).reshape(g * 512, n)


E2M1 = np.array([0.0, 0.5, 1.0, 1.5, 2.0, 3.0, 4.0, 6.0, -0.0, -0.5, -1.0, -1.5, -2.0, -3.0, -4.0, -6.0])


def pack_fp4(w):
    k, n = w.shape
    w = f64(np.asarray(w, np.float32).astype(ml_dtypes.bfloat16)).reshape(k // 32, 32, n)
    amax = np.abs(w).max(1)
    mant, ex = np.frexp(amax / 6.0)
    byte = np.clip(np.where(amax > 0, np.where(mant > 0.5, ex, ex - 1) + 127, 1), 1, 254)
    scaled = (w * np.exp2(127.0 - byte)[:, None, :]).reshape(k, n).astype(np.float32)
    c = np.ascontiguousarray(scaled.reshape(k // 512, 128, 4, n).transpose(0, 1, 3, 2)).astype(ml_dtypes.float4_e2m1fn).view(np.uint8) & 0xF
    words = (c[..., 0::2] | (c[..., 1::2] << 4)).reshape(k // 512, 128, 2 * n)
    return np.ascontiguousarray(words), np.ascontiguousarray(byte.astype(np.uint8).reshape(k // 512, 16, n))


def unpack_fp4(words, scales):
    g, _, n = scales.shape
    words = np.ascontiguousarray(words).reshape(g, 128, n, 2)
    nib = np.empty((g, 128, n, 4), np.uint8)
    nib[..., 0::2] = words & 0xF
    nib[..., 1::2] = words >> 4
    vals = E2M1[nib] * np.repeat(np.exp2(scales.astype(np.float64) - 127.0), 8, axis=1)[..., None]
    return vals.transpose(0, 1, 3, 2).reshape(g * 512, n)


K, T, S, H, W, G, U = 512, 2048, 512, 512, 256, 2048, 1024


def setup_inputs():
    n = np.random.standard_normal
    s = mx_kscale(K)[:, None]
    packed_xT = pack_weight(n((K, T)) * s)
    packed_w1 = pack_fp4(n((K, H)) / np.sqrt(K) / s)
    packed_dT = pack_weight(n((K, G)) / s)
    perm = np.stack([np.random.permutation(U) for _ in range(8)])
    return {
        "x_words": packed_xT[0],
        "x_scales": packed_xT[1],
        "w1_words": packed_w1[0],
        "w1_scales": packed_w1[1],
        "gs": (np.random.uniform(0.5, 1.5, (K, 1)) * s).astype(np.float32),
        "d_words": packed_dT[0],
        "d_scales": packed_dT[1],
        "offs": striped(np.random.permutation(T)[:S]),
        "n1": striped8(np.stack([np.random.permutation(S)[:W] for _ in range(8)])),
        "n2": striped8(np.stack([np.random.permutation(S)[:W] for _ in range(8)])),
        "n3": striped8(np.stack([np.random.permutation(S) for _ in range(8)])),
        "k1": striped8(np.random.randint(0, G, (8, H))),
        "n4": striped8(perm[:, :S]),
        "n5": striped8(perm[:, S:]),
        "n6": striped8(np.stack([np.random.permutation(U) for _ in range(8)])),
    }


def reference(x_words, x_scales, w1_words, w1_scales, gs, d_words, d_scales, offs, n1, n2, n3, k1, n4, n5, n6):
    d_k1 = unpack_weight(d_words, d_scales)[np.arange(K)[:, None], runs(k1, K)]
    xq = unpack_weight(x_words, x_scales)[:, unstriped(offs)]
    y = unpack_fp4(w1_words, w1_scales).T @ xq
    pa = y[np.arange(H)[:, None], runs(n2, H)]
    ds = y.copy()
    ds[np.arange(H)[:, None], runs(n1, H)] = pa
    z = f64(gs) * (ds - (0.5 * (ds[np.arange(H)[:, None], runs(n3, H)])))
    h = 0.0625 * ((d_k1.T @ mxq(z, 0, "e4m3")))
    nw = 0.5 * h
    ph = np.zeros((H, U))
    ph[np.arange(H)[:, None], runs(n4, H)] = h
    pg = ph.copy()
    pg[np.arange(H)[:, None], runs(n5, H)] = nw
    return pg - (pg[np.arange(H)[:, None], runs(n6, H)])

@@ -1,0 +1,162 @@
+from contextlib import ExitStack
+
+import concourse.mybir as mybir
+
+F32 = mybir.dt.float32
+BF16 = mybir.dt.bfloat16
+I32 = mybir.dt.int32
+U32 = mybir.dt.uint32
+U16 = mybir.dt.uint16
+U8 = mybir.dt.uint8
+FP8X4 = mybir.dt.float8_e4m3fn_x4
+FP4X4 = mybir.dt.float4_e2m1fn_x4
+COPY = mybir.ActivationFunctionType.Copy
+ADD = mybir.AluOpType.add
+SUB = mybir.AluOpType.subtract
+
+P = 128
+PACK = 4
+K, T, S, H, W, G, U = 512, 2048, 512, 512, 256, 2048, 1024
+HALF = S // 2
+FLOPS = 2 * K * H * S + 2 * H * H * S
+
+
+def tile_picked_denseksetpagtwo_none_p_kernel(
+    tc, x_words, x_scales, w1_words, w1_scales, gs, d_words, d_scales, offs, n1, n2, n3, k1, n4, n5, n6, out
+):
+    nc = tc.nc
+    with ExitStack() as ctx:
+        lists = ctx.enter_context(tc.tile_pool(name="lists", bufs=1))
+        sb = ctx.enter_context(tc.tile_pool(name="sb", bufs=1))
+        psum = ctx.enter_context(tc.psum_pool(name="psum", bufs=1))
+
+        def load_list(src, name):
+            tile = lists.tile([P, src.shape[1]], U16, name=name)
+            nc.sync.dma_start(tile[:], src)
+            return tile
+
+        x_tab = sb.tile([P, T], U32, name="x_tab")
+        xs_tab = sb.tile([P, T], U8, name="xs_tab")
+        ds_tab = sb.tile([P, G], U8, name="ds_tab")
+        w_raw = sb.tile([P, 2 * H], U8, name="w_raw", tag="w_then_d")
+        ws_raw = sb.tile([P, H], U8, name="ws_raw")
+        ds_plane = sb.tile([P, H], U8, name="ds_plane", align_bytes=64)
+        gain = sb.tile([P, PACK], F32, name="gain")
+
+        nc.gpsimd.memset(ws_raw[:].bitcast(I32), 0)
+        nc.gpsimd.memset(xs_tab[:].bitcast(I32), 0)
+        nc.vector.memset(ds_tab[:].bitcast(I32), 0)
+        nc.vector.memset(ds_plane[:].bitcast(I32), 0)
+
+        offs_t = load_list(offs, "offs_t")
+        nc.sync.dma_start(w_raw[:].bitcast(I32), w1_words[0].bitcast(I32))
+        nc.sync.dma_start(x_tab[:].bitcast(I32), x_words[0].rearrange("p n t -> p (n t)").bitcast(I32))
+        for r in range(4):
+            nc.scalar.dma_start(ws_raw[r:P:32, :].bitcast(I32), w1_scales[0].bitcast(I32)[r:16:4, :])
+        for r in range(4):
+            nc.scalar.dma_start(xs_tab[r:P:32, :].bitcast(I32), x_scales[0].bitcast(I32)[r:16:4, :])
+        nc.sync.dma_start(gain[:], gs.rearrange("(p t) o -> p (t o)", t=PACK))
+        n2_t = load_list(n2, "n2_t")
+        n1_t = load_list(n1, "n1_t")
+        k1_t = load_list(k1, "k1_t")
+        for e in range(2):
+            nc.sync.dma_start(ds_tab[e:P:16, :].bitcast(I32), d_scales[0].bitcast(I32)[e:16:2, :])
+        n3_t = load_list(n3, "n3_t")
+        n4_t = load_list(n4, "n4_t")
+        n5_t = load_list(n5, "n5_t")
+        n6_t = load_list(n6, "n6_t")
+
+        xq_s = sb.tile([P, S], U8, name="xq_s", align_bytes=64)
+        xq = sb.tile([P, S], U32, name="xq", align_bytes=64)
+        nc.vector.tensor_copy(xq_s[:], xs_tab[:].indirect(offs_t[:]))
+        w_deal = sb.tile([P, 2 * H], U8, name="w_deal", align_bytes=64)
+        ws_deal = sb.tile([P, H], U8, name="ws_deal", align_bytes=64)
+        nc.scalar.copy(w_deal[:].bitcast(U16).rearrange("p (t m) -> p m t", t=PACK),
+                       w_raw[:].bitcast(U16).rearrange("p (m t) -> p m t", t=PACK))
+        d_tab = sb.tile([P, G], U32, name="d_tab", tag="w_then_d")
+        nc.sync.dma_start(d_tab[:].bitcast(I32), d_words[0].rearrange("p n t -> p (n t)").bitcast(I32))
+        nc.vector.tensor_copy(ws_deal[:].rearrange("p (t m) -> p m t", t=PACK), ws_raw[:].rearrange("p (m t) -> p m t", t=PACK))
+        nc.vector.tensor_copy(xq[:], x_tab[:].indirect(offs_t[:]))
+
+        dq_s = sb.tile([P, H], U8, name="dq_s")
+        dq_s_deal = sb.tile([P, H], U8, name="dq_s_deal")
+        nc.vector.tensor_copy(dq_s[:], ds_tab[:].indirect(k1_t[:]))
+        nc.vector.tensor_copy(dq_s_deal[:].rearrange("p (t m) -> p m t", t=PACK), dq_s[:].rearrange("p (m t) -> p m t", t=PACK))
+        for r in range(4):
+            nc.sync.dma_start(ds_plane[r:P:32, :].bitcast(I32), dq_s_deal[16 * (r // 2) + r % 2 : P : 32, :].bitcast(I32))
+
+        rows = []
+        picked = []
+        for t in range(PACK):
+            acc = psum.tile([P, S], F32, name="acc1_%d" % t)
+            nc.tensor.matmul_mx(out=acc[:], lhsT=w_deal[:, 256 * t : 256 * (t + 1)].bitcast(FP4X4), lhsT_scale=ws_deal[:, P * t : P * (t + 1)],
+                                rhs=xq[:].bitcast(FP8X4), rhs_scale=xq_s[:], start=True, stop=True)
+            y = sb.tile([P, S], F32, name="y_%d" % t)
+            nc.scalar.activation(y[:], acc[:], COPY, scale=gain[:, t : t + 1])
+            pa = sb.tile([P, W], F32, name="pa_%d" % t, tag="late" if t == PACK - 1 else "pa_%d" % t, align_bytes=64)
+            nc.scalar.activation(pa[:], y[:].indirect(n2_t[:]), COPY)
+            nc.vector.tensor_copy(y[:].indirect(n1_t[:]), pa[:])
+            rows.append(y)
+
+        dq = sb.tile([P, H], U32, name="dq", tag="late", align_bytes=64)
+        dq_deal = sb.tile([P, H], U32, name="dq_deal", align_bytes=64)
+        nc.vector.tensor_copy(dq[:], d_tab[:].indirect(k1_t[:]))
+        nc.vector.tensor_copy(dq_deal[:].rearrange("p (t m) -> p m t", t=PACK), dq[:].rearrange("p (m t) -> p m t", t=PACK))
+
+        z_planes = [sb.tile([P, PACK, HALF], BF16, name="z_planes_%d" % c) for c in range(2)]
+        for t in range(PACK):
+            for c in range(2):
+                cols = slice(HALF * c, HALF * (c + 1))
+                far = sb.tile([P, HALF], F32, name="far_%d_%d" % (t, c))
+                nc.scalar.activation(far[:], rows[t][:].indirect(n3_t[:, 16 * c : 16 * (c + 1)]), COPY, scale=-0.5)
+                engine = nc.vector if t == PACK - 1 else nc.gpsimd
+                engine.tensor_tensor(z_planes[c][:, t, :], rows[t][:, cols], far[:], ADD)
+
+        z_codes = sb.tile([P, S], U32, name="z_codes", align_bytes=64)
+        z_scales = sb.tile([P, S], U8, name="z_scales", align_bytes=64)
+        for c in range(2):
+            cols = slice(HALF * c, HALF * (c + 1))
+            woven = sb.tile([P, HALF, PACK], BF16, name="woven_%d" % c, align_bytes=64)
+            nc.vector.tensor_copy(woven[:], z_planes[c][:].rearrange("p t j -> p j t"))
+            nc.vector.quantize_mx(out=z_codes[:, cols].bitcast(FP8X4), scales=z_scales[:, cols], in_=woven[:].rearrange("p j t -> p (j t)"))
+
+        out_rows = out.rearrange("(p t) w -> t p w", t=PACK)
+        spans = [(t, HALF * c, HALF) for c in range(2) for t in range(2)] + [(t, 0, S) for t in range(2, PACK)]
+        accs = []
+        for t, start, width in spans:
+            cols = slice(start, start + width)
+            acc = psum.tile([P, width], F32, name="acc2_%d_%d" % (t, start), tag="acc1_%d" % t if start else "acc2_%d" % t)
+            nc.tensor.matmul_mx(out=acc[:], lhsT=dq_deal[:, P * t : P * (t + 1)].bitcast(FP8X4), lhsT_scale=ds_plane[:, P * t : P * (t + 1)],
+                                rhs=z_codes[:, cols].bitcast(FP8X4), rhs_scale=z_scales[:, cols], start=True, stop=True)
+            accs.append(acc)
+        full = [sb.tile([P, S], F32, name="full_%d" % t) for t in range(PACK)]
+        halved = [sb.tile([P, S], F32, name="halved_%d" % t) for t in range(PACK)]
+        pages = [sb.tile([P, U], F32, name="page_%d" % t) for t in range(PACK)]
+        for pair in range(2):
+            mine = [(acc, span) for acc, span in zip(accs, spans) if span[0] // 2 == pair]
+            for acc, (t, start, width) in mine:
+                nc.scalar.activation(full[t][:, start : start + width], acc[:], COPY, scale=0.0625)
+            for acc, (t, start, width) in mine:
+                nc.scalar.activation(halved[t][:, start : start + width], acc[:], COPY, scale=0.03125)
+        for pair in range(2):
+            for t, start, width in spans:
+                if t // 2 == pair:
+                    nc.vector.tensor_copy(pages[t][:].indirect(n4_t[:, start // 16 : (start + width) // 16]), full[t][:, start : start + width])
+            for t in (2 * pair, 2 * pair + 1):
+                nc.vector.tensor_copy(pages[t][:].indirect(n5_t[:]), halved[t][:])
+        for t in range(PACK):
+            page = pages[t]
+            last = t == PACK - 1
+            pieces = 4 if last else 2
+            width = U // pieces
+            for c in range(pieces):
+                cols = slice(width * c, width * (c + 1))
+                other = sb.tile([P, width], F32, name="other_%d_%d" % (t, c))
+                window = page[:].indirect(n6_t[:, width // 16 * c : width // 16 * (c + 1)])
+                if last and c == 0:
+                    nc.vector.tensor_copy(other[:], window)
+                else:
+                    nc.scalar.activation(other[:], window, COPY)
+                res = sb.tile([P, width], F32, name="res_%d_%d" % (t, c))
+                (nc.vector if last else nc.gpsimd).tensor_tensor(res[:], page[:, cols], other[:], SUB)
+                nc.sync.dma_start(out_rows[t][:, cols], res[:])

@@ -13,6 +13,7 @@ FP4X4 = mybir.dt.float4_e2m1fn_x4
 COPY = mybir.ActivationFunctionType.Copy
 ADD = mybir.AluOpType.add
 SUB = mybir.AluOpType.subtract
+MULT = mybir.AluOpType.mult
 
 P = 128
 PACK = 4
@@ -37,46 +38,46 @@ def tile_picked_denseksetpagtwo_none_p_kernel(
 
         x_tab = sb.tile([P, T], U32, name="x_tab")
         xs_tab = sb.tile([P, T], U8, name="xs_tab")
-        ds_tab = sb.tile([P, G], U8, name="ds_tab")
+        ds_tab = sb.tile([P, G], U8, name="ds_tab", tag="early", align_bytes=64)
         w_raw = sb.tile([P, 2 * H], U8, name="w_raw", tag="w_then_d")
         ws_raw = sb.tile([P, H], U8, name="ws_raw")
         ds_plane = sb.tile([P, H], U8, name="ds_plane", align_bytes=64)
         gain = sb.tile([P, PACK], F32, name="gain")
 
         nc.gpsimd.memset(ws_raw[:].bitcast(I32), 0)
-        nc.gpsimd.memset(xs_tab[:].bitcast(I32), 0)
+        nc.vector.memset(xs_tab[:].bitcast(I32), 0)
         nc.vector.memset(ds_tab[:].bitcast(I32), 0)
         nc.vector.memset(ds_plane[:].bitcast(I32), 0)
 
+        nc.scalar.dma_start(x_tab[:].bitcast(I32), x_words[0].rearrange("p n t -> p (n t)").bitcast(I32))
         offs_t = load_list(offs, "offs_t")
+        k1_t = load_list(k1, "k1_t")
         nc.sync.dma_start(w_raw[:].bitcast(I32), w1_words[0].bitcast(I32))
-        nc.sync.dma_start(x_tab[:].bitcast(I32), x_words[0].rearrange("p n t -> p (n t)").bitcast(I32))
-        for r in range(4):
-            nc.scalar.dma_start(ws_raw[r:P:32, :].bitcast(I32), w1_scales[0].bitcast(I32)[r:16:4, :])
-        for r in range(4):
-            nc.scalar.dma_start(xs_tab[r:P:32, :].bitcast(I32), x_scales[0].bitcast(I32)[r:16:4, :])
         nc.sync.dma_start(gain[:], gs.rearrange("(p t) o -> p (t o)", t=PACK))
         n2_t = load_list(n2, "n2_t")
         n1_t = load_list(n1, "n1_t")
-        k1_t = load_list(k1, "k1_t")
-        for e in range(2):
-            nc.sync.dma_start(ds_tab[e:P:16, :].bitcast(I32), d_scales[0].bitcast(I32)[e:16:2, :])
         n3_t = load_list(n3, "n3_t")
         n4_t = load_list(n4, "n4_t")
         n5_t = load_list(n5, "n5_t")
         n6_t = load_list(n6, "n6_t")
+        for r in range(4):
+            nc.gpsimd.dma_start(ws_raw[r:P:32, :].bitcast(I32), w1_scales[0].bitcast(I32)[r:16:4, :])
+        for r in range(4):
+            nc.scalar.dma_start(xs_tab[r:P:32, :].bitcast(I32), x_scales[0].bitcast(I32)[r:16:4, :])
+        for e in range(2):
+            (nc.gpsimd if e else nc.scalar).dma_start(ds_tab[e:P:16, :].bitcast(I32), d_scales[0].bitcast(I32)[e:16:2, :])
 
         xq_s = sb.tile([P, S], U8, name="xq_s", align_bytes=64)
         xq = sb.tile([P, S], U32, name="xq", align_bytes=64)
-        nc.vector.tensor_copy(xq_s[:], xs_tab[:].indirect(offs_t[:]))
         w_deal = sb.tile([P, 2 * H], U8, name="w_deal", align_bytes=64)
         ws_deal = sb.tile([P, H], U8, name="ws_deal", align_bytes=64)
         nc.scalar.copy(w_deal[:].bitcast(U16).rearrange("p (t m) -> p m t", t=PACK),
                        w_raw[:].bitcast(U16).rearrange("p (m t) -> p m t", t=PACK))
         d_tab = sb.tile([P, G], U32, name="d_tab", tag="w_then_d")
         nc.sync.dma_start(d_tab[:].bitcast(I32), d_words[0].rearrange("p n t -> p (n t)").bitcast(I32))
-        nc.vector.tensor_copy(ws_deal[:].rearrange("p (t m) -> p m t", t=PACK), ws_raw[:].rearrange("p (m t) -> p m t", t=PACK))
+        nc.gpsimd.tensor_copy(ws_deal[:].rearrange("p (t m) -> p m t", t=PACK), ws_raw[:].rearrange("p (m t) -> p m t", t=PACK))
         nc.vector.tensor_copy(xq[:], x_tab[:].indirect(offs_t[:]))
+        nc.vector.tensor_copy(xq_s[:], xs_tab[:].indirect(offs_t[:]))
 
         dq_s = sb.tile([P, H], U8, name="dq_s")
         dq_s_deal = sb.tile([P, H], U8, name="dq_s_deal")
@@ -85,40 +86,71 @@ def tile_picked_denseksetpagtwo_none_p_kernel(
         for r in range(4):
             nc.sync.dma_start(ds_plane[r:P:32, :].bitcast(I32), dq_s_deal[16 * (r // 2) + r % 2 : P : 32, :].bitcast(I32))
 
-        rows = []
-        picked = []
+        accs = []
         for t in range(PACK):
             acc = psum.tile([P, S], F32, name="acc1_%d" % t)
             nc.tensor.matmul_mx(out=acc[:], lhsT=w_deal[:, 256 * t : 256 * (t + 1)].bitcast(FP4X4), lhsT_scale=ws_deal[:, P * t : P * (t + 1)],
                                 rhs=xq[:].bitcast(FP8X4), rhs_scale=xq_s[:], start=True, stop=True)
-            y = sb.tile([P, S], F32, name="y_%d" % t)
-            nc.scalar.activation(y[:], acc[:], COPY, scale=gain[:, t : t + 1])
-            pa = sb.tile([P, W], F32, name="pa_%d" % t, tag="late" if t == PACK - 1 else "pa_%d" % t, align_bytes=64)
-            nc.scalar.activation(pa[:], y[:].indirect(n2_t[:]), COPY)
-            nc.vector.tensor_copy(y[:].indirect(n1_t[:]), pa[:])
-            rows.append(y)
+            accs.append(acc)
+        rows = [sb.tile([P, S], F32, name="y_%d" % t) for t in range(PACK)]
+        tags = ("early", "pa_1", "pa_2", "late")
+        picked = [sb.tile([P, W], F32, name="pa_%d" % t, tag=tags[t], align_bytes=64) for t in range(PACK)]
+
+        def leave(t):
+            nc.scalar.activation(rows[t][:], accs[t][:], COPY, scale=gain[:, t : t + 1])
+
+        def pick(t):
+            if t == 0:
+                nc.vector.tensor_copy(picked[t][:], rows[t][:].indirect(n2_t[:]))
+            else:
+                nc.scalar.activation(picked[t][:], rows[t][:].indirect(n2_t[:]), COPY)
+
+        leave(0)
+        pick(0)
+        leave(1)
+        for t in range(1, PACK):
+            if t + 1 < PACK:
+                leave(t + 1)
+            pick(t)
+        for t in range(PACK):
+            nc.vector.tensor_copy(rows[t][:].indirect(n1_t[:]), picked[t][:])
 
         dq = sb.tile([P, H], U32, name="dq", tag="late", align_bytes=64)
         dq_deal = sb.tile([P, H], U32, name="dq_deal", align_bytes=64)
         nc.vector.tensor_copy(dq[:], d_tab[:].indirect(k1_t[:]))
-        nc.vector.tensor_copy(dq_deal[:].rearrange("p (t m) -> p m t", t=PACK), dq[:].rearrange("p (m t) -> p m t", t=PACK))
 
         z_planes = [sb.tile([P, PACK, HALF], BF16, name="z_planes_%d" % c) for c in range(2)]
-        for t in range(PACK):
-            for c in range(2):
-                cols = slice(HALF * c, HALF * (c + 1))
-                far = sb.tile([P, HALF], F32, name="far_%d_%d" % (t, c))
-                nc.scalar.activation(far[:], rows[t][:].indirect(n3_t[:, 16 * c : 16 * (c + 1)]), COPY, scale=-0.5)
-                engine = nc.vector if t == PACK - 1 else nc.gpsimd
-                engine.tensor_tensor(z_planes[c][:, t, :], rows[t][:, cols], far[:], ADD)
+        far = {}
+        for t, c in ((0, 0), (1, 0), (2, 0), (0, 1), (3, 0), (1, 1), (2, 1), (3, 1)):
+            if True:
+                far[t, c] = sb.tile([P, HALF], F32, name="far_%d_%d" % (t, c))
+                nc.scalar.activation(far[t, c][:], rows[t][:].indirect(n3_t[:, 16 * c : 16 * (c + 1)]), COPY, scale=-0.5)
+
+        def add_far(engine, t, c):
+            engine.tensor_tensor(z_planes[c][:, t, :], rows[t][:, HALF * c : HALF * (c + 1)], far[t, c][:], ADD)
+
+        for c in range(2):
+            for t in range(PACK - 1):
+                add_far(nc.gpsimd, t, c)
 
         z_codes = sb.tile([P, S], U32, name="z_codes", align_bytes=64)
         z_scales = sb.tile([P, S], U8, name="z_scales", align_bytes=64)
-        for c in range(2):
+        woven = [sb.tile([P, HALF, PACK], BF16, name="woven_%d" % c, align_bytes=64) for c in range(2)]
+
+        def weave(c):
+            nc.vector.tensor_copy(woven[c][:].rearrange("p (j i) t -> p j t i", i=4), z_planes[c][:].rearrange("p t (j i) -> p j t i", i=4))
+
+        def quantize(c):
             cols = slice(HALF * c, HALF * (c + 1))
-            woven = sb.tile([P, HALF, PACK], BF16, name="woven_%d" % c, align_bytes=64)
-            nc.vector.tensor_copy(woven[:], z_planes[c][:].rearrange("p t j -> p j t"))
-            nc.vector.quantize_mx(out=z_codes[:, cols].bitcast(FP8X4), scales=z_scales[:, cols], in_=woven[:].rearrange("p j t -> p (j t)"))
+            nc.vector.quantize_mx(out=z_codes[:, cols].bitcast(FP8X4), scales=z_scales[:, cols], in_=woven[c][:].rearrange("p j t -> p (j t)"))
+
+        add_far(nc.vector, PACK - 1, 0)
+        nc.vector.tensor_copy(dq_deal[:].rearrange("p (t m) -> p m t", t=PACK), dq[:].rearrange("p (m t) -> p m t", t=PACK))
+        weave(0)
+        quantize(0)
+        add_far(nc.vector, PACK - 1, 1)
+        weave(1)
+        quantize(1)
 
         out_rows = out.rearrange("(p t) w -> t p w", t=PACK)
         spans = [(t, HALF * c, HALF) for c in range(2) for t in range(2)] + [(t, 0, S) for t in range(2, PACK)]
@@ -147,16 +179,14 @@ def tile_picked_denseksetpagtwo_none_p_kernel(
         for t in range(PACK):
             page = pages[t]
             last = t == PACK - 1
-            pieces = 4 if last else 2
-            width = U // pieces
-            for c in range(pieces):
-                cols = slice(width * c, width * (c + 1))
-                other = sb.tile([P, width], F32, name="other_%d_%d" % (t, c))
-                window = page[:].indirect(n6_t[:, width // 16 * c : width // 16 * (c + 1)])
-                if last and c == 0:
+            edges = ((0, 512, 1024), (0, 512, 1024), (0, 256, 512, 768, 1024), (0, 384, 768, 1024))[t]
+            for lo, hi in zip(edges, edges[1:]):
+                other = sb.tile([P, hi - lo], F32, name="other_%d_%d" % (t, lo))
+                window = page[:].indirect(n6_t[:, lo // 16 : hi // 16])
+                if last and lo == 0:
                     nc.vector.tensor_copy(other[:], window)
                 else:
                     nc.scalar.activation(other[:], window, COPY)
-                res = sb.tile([P, width], F32, name="res_%d_%d" % (t, c))
-                (nc.vector if last else nc.gpsimd).tensor_tensor(res[:], page[:, cols], other[:], SUB)
-                nc.sync.dma_start(out_rows[t][:, cols], res[:])
+                res = sb.tile([P, hi - lo], F32, name="res_%d_%d" % (t, lo))
+                (nc.vector if last else nc.gpsimd).tensor_tensor(res[:], page[:, lo:hi], other[:], SUB)
+                nc.sync.dma_start(out_rows[t][:, lo:hi], res[:])

@@ -44,28 +44,28 @@ def tile_picked_denseksetpagtwo_none_p_kernel(
         ds_plane = sb.tile([P, H], U8, name="ds_plane", align_bytes=64)
         gain = sb.tile([P, PACK], F32, name="gain")
 
-        nc.gpsimd.memset(ws_raw[:].bitcast(I32), 0)
         nc.vector.memset(xs_tab[:].bitcast(I32), 0)
+        nc.vector.memset(ws_raw[:].bitcast(I32), 0)
         nc.vector.memset(ds_tab[:].bitcast(I32), 0)
-        nc.vector.memset(ds_plane[:].bitcast(I32), 0)
+        nc.gpsimd.memset(ds_plane[:].bitcast(I32), 0)
 
-        nc.scalar.dma_start(x_tab[:].bitcast(I32), x_words[0].rearrange("p n t -> p (n t)").bitcast(I32))
         offs_t = load_list(offs, "offs_t")
         k1_t = load_list(k1, "k1_t")
-        nc.sync.dma_start(w_raw[:].bitcast(I32), w1_words[0].bitcast(I32))
-        nc.sync.dma_start(gain[:], gs.rearrange("(p t) o -> p (t o)", t=PACK))
         n2_t = load_list(n2, "n2_t")
+        nc.scalar.dma_start(gain[:], gs.rearrange("(p t) o -> p (t o)", t=PACK))
         n1_t = load_list(n1, "n1_t")
         n3_t = load_list(n3, "n3_t")
+        nc.scalar.dma_start(w_raw[:].bitcast(I32), w1_words[0].bitcast(I32))
+        nc.sync.dma_start(x_tab[:].bitcast(I32), x_words[0].rearrange("p n t -> p (n t)").bitcast(I32))
         n4_t = load_list(n4, "n4_t")
         n5_t = load_list(n5, "n5_t")
         n6_t = load_list(n6, "n6_t")
         for r in range(4):
-            nc.gpsimd.dma_start(ws_raw[r:P:32, :].bitcast(I32), w1_scales[0].bitcast(I32)[r:16:4, :])
+            nc.sync.dma_start(xs_tab[r:P:32, :].bitcast(I32), x_scales[0].bitcast(I32)[r:16:4, :])
         for r in range(4):
-            nc.scalar.dma_start(xs_tab[r:P:32, :].bitcast(I32), x_scales[0].bitcast(I32)[r:16:4, :])
+            nc.sync.dma_start(ws_raw[r:P:32, :].bitcast(I32), w1_scales[0].bitcast(I32)[r:16:4, :])
         for e in range(2):
-            (nc.gpsimd if e else nc.scalar).dma_start(ds_tab[e:P:16, :].bitcast(I32), d_scales[0].bitcast(I32)[e:16:2, :])
+            nc.sync.dma_start(ds_tab[e:P:16, :].bitcast(I32), d_scales[0].bitcast(I32)[e:16:2, :])
 
         xq_s = sb.tile([P, S], U8, name="xq_s", align_bytes=64)
         xq = sb.tile([P, S], U32, name="xq", align_bytes=64)
@@ -75,9 +75,9 @@ def tile_picked_denseksetpagtwo_none_p_kernel(
                        w_raw[:].bitcast(U16).rearrange("p (m t) -> p m t", t=PACK))
         d_tab = sb.tile([P, G], U32, name="d_tab", tag="w_then_d")
         nc.sync.dma_start(d_tab[:].bitcast(I32), d_words[0].rearrange("p n t -> p (n t)").bitcast(I32))
-        nc.gpsimd.tensor_copy(ws_deal[:].rearrange("p (t m) -> p m t", t=PACK), ws_raw[:].rearrange("p (m t) -> p m t", t=PACK))
         nc.vector.tensor_copy(xq[:], x_tab[:].indirect(offs_t[:]))
         nc.vector.tensor_copy(xq_s[:], xs_tab[:].indirect(offs_t[:]))
+        nc.vector.tensor_copy(ws_deal[:].rearrange("p (t m) -> p m t", t=PACK), ws_raw[:].rearrange("p (m t) -> p m t", t=PACK))
 
         dq_s = sb.tile([P, H], U8, name="dq_s")
         dq_s_deal = sb.tile([P, H], U8, name="dq_s_deal")
@@ -121,16 +121,16 @@ def tile_picked_denseksetpagtwo_none_p_kernel(
 
         z_planes = [sb.tile([P, PACK, HALF], BF16, name="z_planes_%d" % c) for c in range(2)]
         far = {}
-        for t, c in ((0, 0), (1, 0), (2, 0), (0, 1), (3, 0), (1, 1), (2, 1), (3, 1)):
-            if True:
+        for t in range(PACK):
+            for c in range(2):
                 far[t, c] = sb.tile([P, HALF], F32, name="far_%d_%d" % (t, c))
                 nc.scalar.activation(far[t, c][:], rows[t][:].indirect(n3_t[:, 16 * c : 16 * (c + 1)]), COPY, scale=-0.5)
 
         def add_far(engine, t, c):
             engine.tensor_tensor(z_planes[c][:, t, :], rows[t][:, HALF * c : HALF * (c + 1)], far[t, c][:], ADD)
 
-        for c in range(2):
-            for t in range(PACK - 1):
+        for t in range(PACK - 1):
+            for c in range(2):
                 add_far(nc.gpsimd, t, c)
 
         z_codes = sb.tile([P, S], U32, name="z_codes", align_bytes=64)
@@ -147,8 +147,8 @@ def tile_picked_denseksetpagtwo_none_p_kernel(
         add_far(nc.vector, PACK - 1, 0)
         nc.vector.tensor_copy(dq_deal[:].rearrange("p (t m) -> p m t", t=PACK), dq[:].rearrange("p (m t) -> p m t", t=PACK))
         weave(0)
-        quantize(0)
         add_far(nc.vector, PACK - 1, 1)
+        quantize(0)
         weave(1)
         quantize(1)
 

from contextlib import ExitStack

import concourse.mybir as mybir

F32 = mybir.dt.float32
BF16 = mybir.dt.bfloat16
I32 = mybir.dt.int32
U32 = mybir.dt.uint32
U16 = mybir.dt.uint16
U8 = mybir.dt.uint8
FP8X4 = mybir.dt.float8_e4m3fn_x4
FP4X4 = mybir.dt.float4_e2m1fn_x4
COPY = mybir.ActivationFunctionType.Copy
ADD = mybir.AluOpType.add
SUB = mybir.AluOpType.subtract
MULT = mybir.AluOpType.mult

P = 128
PACK = 4
K, T, S, H, W, G, U = 512, 2048, 512, 512, 256, 2048, 1024
HALF = S // 2
FLOPS = 2 * K * H * S + 2 * H * H * S


def tile_picked_denseksetpagtwo_none_p_kernel(
    tc, x_words, x_scales, w1_words, w1_scales, gs, d_words, d_scales, offs, n1, n2, n3, k1, n4, n5, n6, out
):
    nc = tc.nc
    with ExitStack() as ctx:
        lists = ctx.enter_context(tc.tile_pool(name="lists", bufs=1))
        sb = ctx.enter_context(tc.tile_pool(name="sb", bufs=1))
        psum = ctx.enter_context(tc.psum_pool(name="psum", bufs=1))

        def load_list(src, name):
            tile = lists.tile([P, src.shape[1]], U16, name=name)
            nc.sync.dma_start(tile[:], src)
            return tile

        x_tab = sb.tile([P, T], U32, name="x_tab")
        xs_tab = sb.tile([P, T], U8, name="xs_tab")
        ds_tab = sb.tile([P, G], U8, name="ds_tab", tag="early", align_bytes=64)
        w_raw = sb.tile([P, 2 * H], U8, name="w_raw", tag="w_then_d")
        ws_raw = sb.tile([P, H], U8, name="ws_raw")
        ds_plane = sb.tile([P, H], U8, name="ds_plane", align_bytes=64)
        gain = sb.tile([P, PACK], F32, name="gain")

        nc.vector.memset(xs_tab[:].bitcast(I32), 0)
        nc.vector.memset(ws_raw[:].bitcast(I32), 0)
        nc.vector.memset(ds_tab[:].bitcast(I32), 0)
        nc.gpsimd.memset(ds_plane[:].bitcast(I32), 0)

        offs_t = load_list(offs, "offs_t")
        k1_t = load_list(k1, "k1_t")
        n2_t = load_list(n2, "n2_t")
        nc.scalar.dma_start(gain[:], gs.rearrange("(p t) o -> p (t o)", t=PACK))
        n1_t = load_list(n1, "n1_t")
        n3_t = load_list(n3, "n3_t")
        nc.scalar.dma_start(w_raw[:].bitcast(I32), w1_words[0].bitcast(I32))
        nc.sync.dma_start(x_tab[:].bitcast(I32), x_words[0].rearrange("p n t -> p (n t)").bitcast(I32))
        n4_t = load_list(n4, "n4_t")
        n5_t = load_list(n5, "n5_t")
        n6_t = load_list(n6, "n6_t")
        for r in range(4):
            nc.sync.dma_start(xs_tab[r:P:32, :].bitcast(I32), x_scales[0].bitcast(I32)[r:16:4, :])
        for r in range(4):
            nc.sync.dma_start(ws_raw[r:P:32, :].bitcast(I32), w1_scales[0].bitcast(I32)[r:16:4, :])
        for e in range(2):
            nc.sync.dma_start(ds_tab[e:P:16, :].bitcast(I32), d_scales[0].bitcast(I32)[e:16:2, :])

        xq_s = sb.tile([P, S], U8, name="xq_s", align_bytes=64)
        xq = sb.tile([P, S], U32, name="xq", align_bytes=64)
        w_deal = sb.tile([P, 2 * H], U8, name="w_deal", align_bytes=64)
        ws_deal = sb.tile([P, H], U8, name="ws_deal", align_bytes=64)
        nc.scalar.copy(w_deal[:].bitcast(U16).rearrange("p (t m) -> p m t", t=PACK),
                       w_raw[:].bitcast(U16).rearrange("p (m t) -> p m t", t=PACK))
        d_tab = sb.tile([P, G], U32, name="d_tab", tag="w_then_d")
        nc.sync.dma_start(d_tab[:].bitcast(I32), d_words[0].rearrange("p n t -> p (n t)").bitcast(I32))
        nc.vector.tensor_copy(xq[:], x_tab[:].indirect(offs_t[:]))
        nc.vector.tensor_copy(xq_s[:], xs_tab[:].indirect(offs_t[:]))
        nc.vector.tensor_copy(ws_deal[:].rearrange("p (t m) -> p m t", t=PACK), ws_raw[:].rearrange("p (m t) -> p m t", t=PACK))

        dq_s = sb.tile([P, H], U8, name="dq_s")
        dq_s_deal = sb.tile([P, H], U8, name="dq_s_deal")
        nc.vector.tensor_copy(dq_s[:], ds_tab[:].indirect(k1_t[:]))
        nc.vector.tensor_copy(dq_s_deal[:].rearrange("p (t m) -> p m t", t=PACK), dq_s[:].rearrange("p (m t) -> p m t", t=PACK))
        for r in range(4):
            nc.sync.dma_start(ds_plane[r:P:32, :].bitcast(I32), dq_s_deal[16 * (r // 2) + r % 2 : P : 32, :].bitcast(I32))

        accs = []
        for t in range(PACK):
            acc = psum.tile([P, S], F32, name="acc1_%d" % t)
            nc.tensor.matmul_mx(out=acc[:], lhsT=w_deal[:, 256 * t : 256 * (t + 1)].bitcast(FP4X4), lhsT_scale=ws_deal[:, P * t : P * (t + 1)],
                                rhs=xq[:].bitcast(FP8X4), rhs_scale=xq_s[:], start=True, stop=True)
            accs.append(acc)
        rows = [sb.tile([P, S], F32, name="y_%d" % t) for t in range(PACK)]
        tags = ("early", "pa_1", "pa_2", "late")
        picked = [sb.tile([P, W], F32, name="pa_%d" % t, tag=tags[t], align_bytes=64) for t in range(PACK)]

        def leave(t):
            nc.scalar.activation(rows[t][:], accs[t][:], COPY, scale=gain[:, t : t + 1])

        def pick(t):
            if t == 0:
                nc.vector.tensor_copy(picked[t][:], rows[t][:].indirect(n2_t[:]))
            else:
                nc.scalar.activation(picked[t][:], rows[t][:].indirect(n2_t[:]), COPY)

        leave(0)
        pick(0)
        leave(1)
        for t in range(1, PACK):
            if t + 1 < PACK:
                leave(t + 1)
            pick(t)
        for t in range(PACK):
            nc.vector.tensor_copy(rows[t][:].indirect(n1_t[:]), picked[t][:])

        dq = sb.tile([P, H], U32, name="dq", tag="late", align_bytes=64)
        dq_deal = sb.tile([P, H], U32, name="dq_deal", align_bytes=64)
        nc.vector.tensor_copy(dq[:], d_tab[:].indirect(k1_t[:]))

        z_planes = [sb.tile([P, PACK, HALF], BF16, name="z_planes_%d" % c) for c in range(2)]
        far = {}
        for t in range(PACK):
            for c in range(2):
                far[t, c] = sb.tile([P, HALF], F32, name="far_%d_%d" % (t, c))
                nc.scalar.activation(far[t, c][:], rows[t][:].indirect(n3_t[:, 16 * c : 16 * (c + 1)]), COPY, scale=-0.5)

        def add_far(engine, t, c):
            engine.tensor_tensor(z_planes[c][:, t, :], rows[t][:, HALF * c : HALF * (c + 1)], far[t, c][:], ADD)

        for t in range(PACK - 1):
            for c in range(2):
                add_far(nc.gpsimd, t, c)

        z_codes = sb.tile([P, S], U32, name="z_codes", align_bytes=64)
        z_scales = sb.tile([P, S], U8, name="z_scales", align_bytes=64)
        woven = [sb.tile([P, HALF, PACK], BF16, name="woven_%d" % c, align_bytes=64) for c in range(2)]

        def weave(c):
            nc.vector.tensor_copy(woven[c][:].rearrange("p (j i) t -> p j t i", i=4), z_planes[c][:].rearrange("p t (j i) -> p j t i", i=4))

        def quantize(c):
            cols = slice(HALF * c, HALF * (c + 1))
            nc.vector.quantize_mx(out=z_codes[:, cols].bitcast(FP8X4), scales=z_scales[:, cols], in_=woven[c][:].rearrange("p j t -> p (j t)"))

        add_far(nc.vector, PACK - 1, 0)
        nc.vector.tensor_copy(dq_deal[:].rearrange("p (t m) -> p m t", t=PACK), dq[:].rearrange("p (m t) -> p m t", t=PACK))
        weave(0)
        add_far(nc.vector, PACK - 1, 1)
        quantize(0)
        weave(1)
        quantize(1)

        out_rows = out.rearrange("(p t) w -> t p w", t=PACK)
        spans = [(t, HALF * c, HALF) for c in range(2) for t in range(2)] + [(t, 0, S) for t in range(2, PACK)]
        accs = []
        for t, start, width in spans:
            cols = slice(start, start + width)
            acc = psum.tile([P, width], F32, name="acc2_%d_%d" % (t, start), tag="acc1_%d" % t if start else "acc2_%d" % t)
            nc.tensor.matmul_mx(out=acc[:], lhsT=dq_deal[:, P * t : P * (t + 1)].bitcast(FP8X4), lhsT_scale=ds_plane[:, P * t : P * (t + 1)],
                                rhs=z_codes[:, cols].bitcast(FP8X4), rhs_scale=z_scales[:, cols], start=True, stop=True)
            accs.append(acc)
        full = [sb.tile([P, S], F32, name="full_%d" % t) for t in range(PACK)]
        halved = [sb.tile([P, S], F32, name="halved_%d" % t) for t in range(PACK)]
        pages = [sb.tile([P, U], F32, name="page_%d" % t) for t in range(PACK)]
        for pair in range(2):
            mine = [(acc, span) for acc, span in zip(accs, spans) if span[0] // 2 == pair]
            for acc, (t, start, width) in mine:
                nc.scalar.activation(full[t][:, start : start + width], acc[:], COPY, scale=0.0625)
            for acc, (t, start, width) in mine:
                nc.scalar.activation(halved[t][:, start : start + width], acc[:], COPY, scale=0.03125)
        for pair in range(2):
            for t, start, width in spans:
                if t // 2 == pair:
                    nc.vector.tensor_copy(pages[t][:].indirect(n4_t[:, start // 16 : (start + width) // 16]), full[t][:, start : start + width])
            for t in (2 * pair, 2 * pair + 1):
                nc.vector.tensor_copy(pages[t][:].indirect(n5_t[:]), halved[t][:])
        for t in range(PACK):
            page = pages[t]
            last = t == PACK - 1
            edges = ((0, 512, 1024), (0, 512, 1024), (0, 256, 512, 768, 1024), (0, 384, 768, 1024))[t]
            for lo, hi in zip(edges, edges[1:]):
                other = sb.tile([P, hi - lo], F32, name="other_%d_%d" % (t, lo))
                window = page[:].indirect(n6_t[:, lo // 16 : hi // 16])
                if last and lo == 0:
                    nc.vector.tensor_copy(other[:], window)
                else:
                    nc.scalar.activation(other[:], window, COPY)
                res = sb.tile([P, hi - lo], F32, name="res_%d_%d" % (t, lo))
                (nc.vector if last else nc.gpsimd).tensor_tensor(res[:], page[:, lo:hi], other[:], SUB)
                nc.sync.dma_start(out_rows[t][:, lo:hi], res[:])
